import numpy as np
import ml_dtypes


def mxq(x, axis, fmt="e4m3"):
    dtype, down = {"e4m3": (ml_dtypes.float8_e4m3fn, 7), "e5m2": (ml_dtypes.float8_e5m2, 14)}[fmt]
    v = np.moveaxis(np.asarray(x, np.float32).astype(ml_dtypes.bfloat16).astype(np.float64), axis, -1)
    blocks = v.reshape(v.shape[:-1] + (-1, 32))
    amax = np.abs(blocks).max(-1, keepdims=True)
    byte = np.maximum(np.where(amax > 0, np.frexp(amax)[1] - 1 + 127, 0) - down, 1)
    scale = np.exp2(byte - 127.0)
    codes = (blocks / scale).astype(np.float32).astype(dtype).astype(np.float64)
    return np.moveaxis((codes * scale).reshape(v.shape), -1, axis)


WIDE = False


def mx_kscale(k):
    if not WIDE:
        return np.ones(k)
    levels = np.array([10, -10, 5, -5, 0])
    if k % 512:
        return np.exp2(np.random.permutation(np.resize(levels, k // 32))).repeat(32)
    a = np.empty((k // 512, 16))
    for p in range(k // 512):
        a[p, :8] = np.random.permutation(np.resize(levels, 8))
        for g in range(8):
            far = levels[np.abs(levels - a[p, g]) >= 10]
            a[p, g + 8] = far[np.random.randint(len(far))]
    return np.exp2(a.ravel()).repeat(32)


def f64(x):
    return np.asarray(x).astype(np.float64)


def striped(idx):
    return np.tile(idx.reshape(-1, 16).T, (8, 1)).astype(np.uint16)


def unstriped(offs):
    return offs[:16].T.reshape(-1).astype(np.int64)


E2M1 = np.array([0.0, 0.5, 1.0, 1.5, 2.0, 3.0, 4.0, 6.0, -0.0, -0.5, -1.0, -1.5, -2.0, -3.0, -4.0, -6.0])


def pack_weight(w, fmt):
    k, n = w.shape
    w = f64(np.asarray(w, np.float32).astype(ml_dtypes.bfloat16)).reshape(k // 32, 32, n)
    amax = np.abs(w).max(1)
    if fmt == "e4m3":
        byte = np.frexp(amax)[1] - 1 + 127 - 7
    else:
        mant, ex = np.frexp(amax / 6.0)
        byte = np.where(mant > 0.5, ex, ex - 1) + 127
    byte = np.clip(np.where(amax > 0, byte, 1), 1, 254)
    scaled = (w * np.exp2(127.0 - byte)[:, None, :]).reshape(k, n).astype(np.float32)
    by_word = np.ascontiguousarray(scaled.reshape(k // 512, 128, 4, n).transpose(0, 1, 3, 2))
    if fmt == "e4m3":
        words = by_word.astype(ml_dtypes.float8_e4m3fn).view(np.uint8)
    else:
        c = by_word.astype(ml_dtypes.float4_e2m1fn).view(np.uint8) & 0xF
        words = (c[..., 0::2] | (c[..., 1::2] << 4)).reshape(k // 512, 128, 2 * n)
    return np.ascontiguousarray(words), np.ascontiguousarray(byte.astype(np.uint8).reshape(k // 512, 16, n))


def unpack_weight(words, scales, fmt):
    g, _, n = scales.shape
    words = np.ascontiguousarray(words).reshape(g, 128, n, -1)
    if fmt == "e4m3":
        vals = words.view(ml_dtypes.float8_e4m3fn).astype(np.float64)
    else:
        nib = np.empty((g, 128, n, 4), np.uint8)
        nib[..., 0::2] = words & 0xF
        nib[..., 1::2] = words >> 4
        vals = E2M1[nib]
    vals = vals * np.repeat(np.exp2(scales.astype(np.float64) - 127.0), 8, axis=1)[..., None]
    return vals.transpose(0, 1, 3, 2).reshape(g * 512, n)


def gelu(v):
    return 0.5 * v * (1.0 + np.tanh(np.sqrt(2.0 / np.pi) * (v + 0.044715 * v**3)))


K, K2, H, N, T, S = 512, 1024, 1024, 512, 2048, 1024

def setup_inputs():
    n = np.random.standard_normal
    s = mx_kscale(K)[:, None]
    s2 = mx_kscale(K2)[:, None]
    u = mx_kscale(H)[:, None]
    tab_words, tab_scales = pack_weight(n((K, T)) * s, "e4m3")
    tab2_words, tab2_scales = pack_weight(n((K2, T)) * s2, "e4m3")
    wa_words, wa_scales = pack_weight(0.7 * n((K, H)) / np.sqrt(K) / s, "e2m1")
    wb = 0.7 * n((K2, H)) / np.sqrt(K2) / s2
    gain = np.exp(0.3 * n(H)) * u[:, 0]
    w = n((H, N)) / np.sqrt(H) / u
    gT = 0.7 * n((N, T))
    return {
        "tab_words": tab_words, "tab_scales": tab_scales,
        "tab2_words": tab2_words, "tab2_scales": tab2_scales,
        "wa_words": wa_words, "wa_scales": wa_scales,
        "wb": wb.astype(np.float32), "gain": gain.astype(np.float32),
        "w": w.astype(np.float32), "gT": gT.astype(np.float32),
        "offs": striped(np.random.permutation(T)[:S]),
        "offs2": striped(np.random.permutation(T)[:S]),
    }

def reference(tab_words, tab_scales, tab2_words, tab2_scales, wa_words, wa_scales, wb, gain, w, gT, offs, offs2):
    v = unpack_weight(tab_words, tab_scales, "e4m3")[:, unstriped(offs)]
    v2 = unpack_weight(tab2_words, tab2_scales, "e4m3")[:, unstriped(offs2)]
    g = f64(gT)[:, unstriped(offs)]
    wa = unpack_weight(wa_words, wa_scales, "e2m1")
    a = wa.T @ v + mxq(f64(wb), 0, "e4m3").T @ v2
    h = np.square(a) * f64(gain)[:, None]
    y = mxq(f64(w), 0, "e4m3").T @ mxq(h, 0, "e4m3")
    return y - g

@@ -1,0 +1,273 @@
+from contextlib import ExitStack
+
+import concourse.mybir as mybir
+
+K, K2, H, N, T, S = 512, 1024, 1024, 512, 2048, 1024
+FLOPS = 2 * S * (K * H + K2 * H + H * N)
+
+F32 = mybir.dt.float32
+BF16 = mybir.dt.bfloat16
+I32 = mybir.dt.int32
+U32 = mybir.dt.uint32
+U16 = mybir.dt.uint16
+U8 = mybir.dt.uint8
+FP8X4 = mybir.dt.float8_e4m3fn_x4
+FP4X4 = mybir.dt.float4_e2m1fn_x4
+ALU = mybir.AluOpType
+ACT = mybir.ActivationFunctionType
+
+P = 128
+PACK = 4
+PASS = P * PACK
+COLS = 512
+HALVES = S // COLS
+ROOT_FLOOR = 2.0**-100
+
+
+def tile_list_squared_factor_match_kernel(
+    tc, tab_words, tab_scales, tab2_words, tab2_scales, wa_words, wa_scales, wb, gain, w, gT, offs, offs2, out
+):
+    nc = tc.nc
+    with ExitStack() as ctx:
+        keep = ctx.enter_context(tc.tile_pool(name="keep", bufs=1))
+        ring = ctx.enter_context(tc.tile_pool(name="ring", bufs=3))
+        psum = ctx.enter_context(tc.psum_pool(name="psum", bufs=8))
+
+        def held(name, shape, dtype):
+            return keep.tile(shape, dtype, name=name, align_bytes=64)
+
+        idx = held("idx", [P, S // 16], U16)
+        idx2 = held("idx2", [P, S // 16], U16)
+        gain_sb = held("gain_sb", [P, H // PASS, PACK], F32)
+        v_rows = held("v_rows", [P, T // 4], I32)
+        v2_rows = held("v2_rows", [P, T // 4], I32)
+        wa_rows = held("wa_rows", [P, H // 4], I32)
+        v_tab = held("v_tab", [P, T], I32)
+        v2_tab = [held(f"v2_tab{a}", [P, T], I32) for a in range(2)]
+        wa_raw = held("wa_raw", [P, H // 2], I32)
+        wb_raw = {(a, b): held(f"wb_raw{a}{b}", [P, PACK, PASS], F32) for a in range(2) for b in range(2)}
+        w_raw = [held(f"w_raw{b}", [P, PACK, N], F32) for b in range(2)]
+        g_tab = [held(f"g_tab{n}", [P, T], F32) for n in range(4)]
+
+        def half_of(offsets, jh):
+            return offsets[:, jh * (COLS // 16) : (jh + 1) * (COLS // 16)]
+
+        def load_words(tile, words):
+            nc.sync.dma_start(tile[:], words.rearrange("p n t -> p (n t)").bitcast(I32))
+
+        def load_scales(tile, rows, first, queue):
+            passes = rows.shape[0]
+            for q in range(4):
+                lo = 32 * q + first
+                queue.dma_start(tile[lo : lo + 4 * passes, :], rows.bitcast(I32)[:, 4 * q : 4 * q + 4, :])
+
+        def load_wb(a, b):
+            rows = wb[a * PASS : (a + 1) * PASS, b * PASS : (b + 1) * PASS]
+            nc.sync.dma_start(wb_raw[a, b][:], rows.rearrange("(p j) c -> p j c", j=PACK))
+
+        def load_w(b):
+            nc.sync.dma_start(w_raw[b][:], w[b * PASS : (b + 1) * PASS, :].rearrange("(p j) c -> p j c", j=PACK))
+
+        def load_g(n):
+            nc.sync.dma_start(g_tab[n][:], gT[n * P : (n + 1) * P, :])
+
+        def gather(name, window, offsets, jh, dtype):
+            tile = held(f"{name}{jh}", [P, COLS], dtype)
+            nc.vector.tensor_copy(tile[:], window.indirect(half_of(offsets, jh)))
+            return tile
+
+        def quantise(name, grouped):
+            codes = held(name + "_codes", [P, COLS], U32)
+            scales = held(name + "_scales", [P, COLS], U8)
+            nc.vector.quantize_mx(out=codes[:].bitcast(FP8X4), scales=scales[:], in_=grouped[:])
+            return codes, scales
+
+        def shared_copy(dst, src, on_vector):
+            if on_vector > 0:
+                nc.vector.tensor_copy(dst[:, :on_vector], src[:, :on_vector])
+            if on_vector < P:
+                nc.scalar.copy(out=dst[:, on_vector:], in_=src[:, on_vector:])
+
+        def round_wb(a, b, on_vector):
+            grouped = ring.tile([P, PACK * PASS], BF16, name="grouped", align_bytes=64, bufs=4)
+            shared_copy(
+                grouped[:].rearrange("p (t m j) -> p m j t", t=PACK, j=PACK),
+                wb_raw[a, b][:].rearrange("p j (m t) -> p m j t", t=PACK),
+                on_vector,
+            )
+            return grouped
+
+        def round_w(b, how, on_vector):
+            grouped = ring.tile([P, PACK * N], BF16, name="grouped", align_bytes=64, bufs=4)
+            dst = grouped[:].rearrange("p (c i j) -> p c j i", i=4, j=PACK)
+            if how == "V":
+                nc.vector.tensor_tensor(
+                    dst,
+                    w_raw[b][:].rearrange("p j (c i) -> p c j i", i=4),
+                    sign[:, b, :].unsqueeze(1).unsqueeze(3).to_broadcast([P, N // 4, PACK, 4]),
+                    ALU.mult,
+                )
+                return grouped
+            signed = ring.tile([P, PACK, N], BF16, name="signed", align_bytes=64, bufs=2)
+            for j in range(PACK):
+                if how == "G":
+                    nc.gpsimd.tensor_scalar(signed[:, j, :], w_raw[b][:, j, :], sign[:, b, j : j + 1], 0.0, ALU.mult, ALU.add)
+                else:
+                    nc.scalar.activation(signed[:, j, :], w_raw[b][:, j, :], ACT.Copy, scale=sign[:, b, j : j + 1])
+            shared_copy(dst, signed[:].rearrange("p j (c i) -> p c j i", i=4), on_vector)
+            return grouped
+
+        def factors(b, jh):
+            planes = ring.tile([P, PACK, COLS], BF16, name="planes", align_bytes=64)
+            for t in range(PACK):
+                acc = psum.tile([P, COLS], F32, name="acc")
+                col = (b * PACK + t) * P
+                nc.tensor.matmul_mx(
+                    out=acc[:],
+                    lhsT=wa_codes[:, 2 * col : 2 * (col + P)].bitcast(FP4X4),
+                    lhsT_scale=wa_sc[:, col : col + P],
+                    rhs=v_codes[jh][:].bitcast(FP8X4),
+                    rhs_scale=v_sc[jh][:],
+                    start=True,
+                    stop=False,
+                )
+                for a in range(2):
+                    codes, scales = wb_q[a, b]
+                    nc.tensor.matmul_mx(
+                        out=acc[:],
+                        lhsT=codes[:, t * P : (t + 1) * P].bitcast(FP8X4),
+                        lhsT_scale=scales[:, t * P : (t + 1) * P],
+                        rhs=v2_codes[a, jh][:].bitcast(FP8X4),
+                        rhs_scale=v2_sc[jh][4 + 4 * a :, :],
+                        start=False,
+                        stop=(a == 1),
+                    )
+                nc.scalar.activation(planes[:, t, :], acc[:], ACT.Square, scale=root[:, b, t : t + 1])
+            return planes
+
+        def interleave(planes, on_vector):
+            grouped = ring.tile([P, PACK * COLS], BF16, name="h_grouped", align_bytes=64)
+            dst = grouped[:].rearrange("p (c i t) -> p c t i", i=4, t=PACK)
+            src = planes[:].rearrange("p t (c i) -> p c t i", i=4)
+            shared_copy(dst, src, on_vector)
+            return grouped
+
+        def finish(n, jh):
+            acc = psum.tile([P, COLS], F32, name="acc")
+            for b in range(2):
+                w_codes, w_scales = w_q[b]
+                h_codes, h_scales = h_q[b, jh]
+                nc.tensor.matmul_mx(
+                    out=acc[:],
+                    lhsT=w_codes[:, n * P : (n + 1) * P].bitcast(FP8X4),
+                    lhsT_scale=w_scales[:, n * P : (n + 1) * P],
+                    rhs=h_codes[:].bitcast(FP8X4),
+                    rhs_scale=h_scales[:],
+                    start=(b == 0),
+                    stop=(b == 1),
+                )
+            result = g_picked[n, jh]
+            nc.vector.tensor_tensor(result[:], acc[:], result[:], ALU.subtract)
+            nc.sync.dma_start(out[n * P : (n + 1) * P, jh * COLS : (jh + 1) * COLS], result[:])
+
+        shape = [P, H // PASS, PACK]
+        sign = held("sign", shape, F32)
+        minus = held("minus", shape, F32)
+        size = held("size", shape, F32)
+        floor = held("floor", shape, F32)
+        guess = held("guess", shape, F32)
+        inverse = held("inverse", shape, F32)
+        half_ratio = held("half_ratio", shape, F32)
+        root = held("root", shape, F32)
+        wa_codes = held("wa_codes", [P, 2 * H], U8)
+        wa_sc = held("wa_sc", [P, H], U8)
+        v_sc, v_codes, v2_sc, v2_codes, wb_q, w_q, h_q, g_picked, wb_g, w_g, h_p, h_g = ({} for each in range(12))
+        nc.vector.memset(v_rows[:], 0)
+        nc.vector.memset(v2_rows[:], 0)
+        nc.vector.memset(wa_rows[:], 0)
+        nc.sync.dma_start(wa_raw[:], wa_words[0].bitcast(I32))
+        nc.sync.dma_start(idx[:], offs)
+        nc.sync.dma_start(idx2[:], offs2)
+        load_scales(v_rows, tab_scales, 0, nc.sync)
+        load_wb(0, 0)
+        load_scales(v2_rows, tab2_scales, 4, nc.sync)
+        load_words(v_tab, tab_words[0])
+        nc.sync.dma_start(gain_sb[:], gain.rearrange("(b p t) -> p b t", p=P, t=PACK))
+        load_wb(0, 1)
+        load_scales(wa_rows, wa_scales, 0, nc.sync)
+        load_wb(1, 1)
+        load_w(0)
+        load_words(v2_tab[0], tab2_words[0])
+        load_words(v2_tab[1], tab2_words[1])
+        load_wb(1, 0)
+        load_g(1)
+        load_g(2)
+        load_w(1)
+        load_g(3)
+        load_g(0)
+        nc.gpsimd.tensor_scalar(minus[:], gain_sb[:], 0.0, -2.0, ALU.is_lt, ALU.mult)
+        nc.gpsimd.tensor_scalar(sign[:], minus[:], 1.0, None, ALU.add)
+        nc.gpsimd.tensor_tensor(size[:], gain_sb[:], sign[:], ALU.mult)
+        nc.gpsimd.tensor_scalar(floor[:], size[:], ROOT_FLOOR, None, ALU.max)
+        nc.scalar.activation(guess[:], floor[:], ACT.Sqrt)
+        wb_g[0, 0] = round_wb(0, 0, 128)
+        g_picked[2, 0] = gather("g2_", g_tab[2][:], idx, 0, F32)
+        v2_codes[1, 0] = gather("v2_codes1", v2_tab[1][:].bitcast(U32), idx2, 0, U32)
+        v_codes[0] = gather("v_codes", v_tab[:].bitcast(U32), idx, 0, U32)
+        nc.vector.reciprocal(inverse[:], guess[:])
+        wb_g[0, 1] = round_wb(0, 1, 0)
+        wb_g[1, 1] = round_wb(1, 1, 0)
+        nc.vector.tensor_copy(
+            wa_sc[:].rearrange("p (b t m) -> p b t m", t=PACK, m=P),
+            wa_rows[:].bitcast(U8).rearrange("p (b m t) -> p b t m", t=PACK, m=P),
+        )
+        nc.vector.scalar_tensor_tensor(half_ratio[:], size[:], 0.5, inverse[:], ALU.mult, ALU.mult)
+        wb_g[1, 0] = round_wb(1, 0, 128)
+        w_g[0] = round_w(0, "G", 0)
+        g_picked[0, 1] = gather("g0_", g_tab[0][:], idx, 1, F32)
+        w_g[1] = round_w(1, "G", 0)
+        g_picked[1, 0] = gather("g1_", g_tab[1][:], idx, 0, F32)
+        w_q[1] = quantise("w1", w_g[1])
+        wb_q[1, 1] = quantise("wb11", wb_g[1, 1])
+        v_sc[0] = gather("v_sc", v_rows[:].bitcast(U8), idx, 0, U8)
+        v2_sc[1] = gather("v2_sc", v2_rows[:].bitcast(U8), idx2, 1, U8)
+        g_picked[3, 1] = gather("g3_", g_tab[3][:], idx, 1, F32)
+        v2_codes[1, 1] = gather("v2_codes1", v2_tab[1][:].bitcast(U32), idx2, 1, U32)
+        v2_codes[0, 0] = gather("v2_codes0", v2_tab[0][:].bitcast(U32), idx2, 0, U32)
+        wb_q[1, 0] = quantise("wb10", wb_g[1, 0])
+        v2_codes[0, 1] = gather("v2_codes0", v2_tab[0][:].bitcast(U32), idx2, 1, U32)
+        wb_q[0, 1] = quantise("wb01", wb_g[0, 1])
+        nc.vector.tensor_copy(
+            wa_codes[:].bitcast(U16).rearrange("p (b t m) -> p b t m", t=PACK, m=P),
+            wa_raw[:].bitcast(U16).rearrange("p (b m t) -> p b t m", t=PACK, m=P),
+        )
+        v2_sc[0] = gather("v2_sc", v2_rows[:].bitcast(U8), idx2, 0, U8)
+        g_picked[2, 1] = gather("g2_", g_tab[2][:], idx, 1, F32)
+        v_sc[1] = gather("v_sc", v_rows[:].bitcast(U8), idx, 1, U8)
+        nc.vector.scalar_tensor_tensor(root[:], guess[:], 0.5, half_ratio[:], ALU.mult, ALU.add)
+        h_p[1, 0] = factors(1, 0)
+        wb_q[0, 0] = quantise("wb00", wb_g[0, 0])
+        v_codes[1] = gather("v_codes", v_tab[:].bitcast(U32), idx, 1, U32)
+        h_p[1, 1] = factors(1, 1)
+        h_p[0, 1] = factors(0, 1)
+        w_q[0] = quantise("w0", w_g[0])
+        h_g[1, 0] = interleave(h_p[1, 0], 96)
+        h_g[1, 1] = interleave(h_p[1, 1], 96)
+        h_q[1, 1] = quantise("h11", h_g[1, 1])
+        h_g[0, 1] = interleave(h_p[0, 1], 32)
+        h_p[0, 0] = factors(0, 0)
+        h_g[0, 0] = interleave(h_p[0, 0], 0)
+        g_picked[3, 0] = gather("g3_", g_tab[3][:], idx, 0, F32)
+        h_q[0, 1] = quantise("h01", h_g[0, 1])
+        finish(3, 1)
+        g_picked[1, 1] = gather("g1_", g_tab[1][:], idx, 1, F32)
+        h_q[1, 0] = quantise("h10", h_g[1, 0])
+        h_q[0, 0] = quantise("h00", h_g[0, 0])
+        finish(1, 0)
+        finish(2, 0)
+        g_picked[0, 0] = gather("g0_", g_tab[0][:], idx, 0, F32)
+        finish(0, 1)
+        finish(1, 1)
+        finish(0, 0)
+        finish(2, 1)
+        finish(3, 0)

@@ -30,7 +30,8 @@ def tile_list_squared_factor_match_kernel(
     nc = tc.nc
     with ExitStack() as ctx:
         keep = ctx.enter_context(tc.tile_pool(name="keep", bufs=1))
-        ring = ctx.enter_context(tc.tile_pool(name="ring", bufs=3))
+        ring = ctx.enter_context(tc.tile_pool(name="ring", bufs=12))
+        line = ctx.enter_context(tc.tile_pool(name="line", bufs=30))
         psum = ctx.enter_context(tc.psum_pool(name="psum", bufs=8))
 
         def held(name, shape, dtype):
@@ -72,12 +73,12 @@ def tile_list_squared_factor_match_kernel(
             nc.sync.dma_start(g_tab[n][:], gT[n * P : (n + 1) * P, :])
 
         def gather(name, window, offsets, jh, dtype):
-            tile = held(f"{name}{jh}", [P, COLS], dtype)
+            tile = line.tile([P, COLS], dtype, name=f"{name}{jh}", tag="vout", align_bytes=64)
             nc.vector.tensor_copy(tile[:], window.indirect(half_of(offsets, jh)))
             return tile
 
         def quantise(name, grouped):
-            codes = held(name + "_codes", [P, COLS], U32)
+            codes = line.tile([P, COLS], U32, name=name + "_codes", tag="vout", align_bytes=64)
             scales = held(name + "_scales", [P, COLS], U8)
             nc.vector.quantize_mx(out=codes[:].bitcast(FP8X4), scales=scales[:], in_=grouped[:])
             return codes, scales
@@ -89,7 +90,7 @@ def tile_list_squared_factor_match_kernel(
                 nc.scalar.copy(out=dst[:, on_vector:], in_=src[:, on_vector:])
 
         def round_wb(a, b, on_vector):
-            grouped = ring.tile([P, PACK * PASS], BF16, name="grouped", align_bytes=64, bufs=4)
+            grouped = ring.tile([P, PACK * PASS], BF16, name="grouped", tag="stage", align_bytes=64)
             shared_copy(
                 grouped[:].rearrange("p (t m j) -> p m j t", t=PACK, j=PACK),
                 wb_raw[a, b][:].rearrange("p j (m t) -> p m j t", t=PACK),
@@ -98,27 +99,25 @@ def tile_list_squared_factor_match_kernel(
             return grouped
 
         def round_w(b, how, on_vector):
-            grouped = ring.tile([P, PACK * N], BF16, name="grouped", align_bytes=64, bufs=4)
-            dst = grouped[:].rearrange("p (c i j) -> p c j i", i=4, j=PACK)
             if how == "V":
+                grouped = ring.tile([P, PACK * N], BF16, name="grouped", tag="stage", align_bytes=64)
                 nc.vector.tensor_tensor(
-                    dst,
+                    grouped[:].rearrange("p (c i j) -> p c j i", i=4, j=PACK),
                     w_raw[b][:].rearrange("p j (c i) -> p c j i", i=4),
                     sign[:, b, :].unsqueeze(1).unsqueeze(3).to_broadcast([P, N // 4, PACK, 4]),
                     ALU.mult,
                 )
                 return grouped
-            signed = ring.tile([P, PACK, N], BF16, name="signed", align_bytes=64, bufs=2)
+            signed = ring.tile([P, PACK, N], BF16, name="signed", tag="stage", align_bytes=64)
             for j in range(PACK):
-                if how == "G":
-                    nc.gpsimd.tensor_scalar(signed[:, j, :], w_raw[b][:, j, :], sign[:, b, j : j + 1], 0.0, ALU.mult, ALU.add)
-                else:
-                    nc.scalar.activation(signed[:, j, :], w_raw[b][:, j, :], ACT.Copy, scale=sign[:, b, j : j + 1])
+                nc.scalar.activation(signed[:, j, :], w_raw[b][:, j, :], ACT.Copy, scale=sign[:, b, j : j + 1])
+            grouped = ring.tile([P, PACK * N], BF16, name="grouped", tag="stage", align_bytes=64)
+            dst = grouped[:].rearrange("p (c i j) -> p c j i", i=4, j=PACK)
             shared_copy(dst, signed[:].rearrange("p j (c i) -> p c j i", i=4), on_vector)
             return grouped
 
         def factors(b, jh):
-            planes = ring.tile([P, PACK, COLS], BF16, name="planes", align_bytes=64)
+            planes = ring.tile([P, PACK, COLS], BF16, name="planes", tag="stage", align_bytes=64)
             for t in range(PACK):
                 acc = psum.tile([P, COLS], F32, name="acc")
                 col = (b * PACK + t) * P
@@ -146,7 +145,7 @@ def tile_list_squared_factor_match_kernel(
             return planes
 
         def interleave(planes, on_vector):
-            grouped = ring.tile([P, PACK * COLS], BF16, name="h_grouped", align_bytes=64)
+            grouped = ring.tile([P, PACK * COLS], BF16, name="h_grouped", tag="stage", align_bytes=64)
             dst = grouped[:].rearrange("p (c i t) -> p c t i", i=4, t=PACK)
             src = planes[:].rearrange("p t (c i) -> p c t i", i=4)
             shared_copy(dst, src, on_vector)
@@ -174,100 +173,98 @@ def tile_list_squared_factor_match_kernel(
         sign = held("sign", shape, F32)
         minus = held("minus", shape, F32)
         size = held("size", shape, F32)
-        floor = held("floor", shape, F32)
         guess = held("guess", shape, F32)
         inverse = held("inverse", shape, F32)
         half_ratio = held("half_ratio", shape, F32)
         root = held("root", shape, F32)
-        wa_codes = held("wa_codes", [P, 2 * H], U8)
-        wa_sc = held("wa_sc", [P, H], U8)
         v_sc, v_codes, v2_sc, v2_codes, wb_q, w_q, h_q, g_picked, wb_g, w_g, h_p, h_g = ({} for each in range(12))
         nc.vector.memset(v_rows[:], 0)
         nc.vector.memset(v2_rows[:], 0)
         nc.vector.memset(wa_rows[:], 0)
-        nc.sync.dma_start(wa_raw[:], wa_words[0].bitcast(I32))
         nc.sync.dma_start(idx[:], offs)
-        nc.sync.dma_start(idx2[:], offs2)
+        nc.sync.dma_start(gain_sb[:], gain.rearrange("(b p t) -> p b t", p=P, t=PACK))
+        load_scales(wa_rows, wa_scales, 0, nc.sync)
+        load_words(v_tab, tab_words[0])
+        load_wb(1, 1)
         load_scales(v_rows, tab_scales, 0, nc.sync)
         load_wb(0, 0)
+        nc.sync.dma_start(idx2[:], offs2)
         load_scales(v2_rows, tab2_scales, 4, nc.sync)
-        load_words(v_tab, tab_words[0])
-        nc.sync.dma_start(gain_sb[:], gain.rearrange("(b p t) -> p b t", p=P, t=PACK))
-        load_wb(0, 1)
-        load_scales(wa_rows, wa_scales, 0, nc.sync)
-        load_wb(1, 1)
-        load_w(0)
+        nc.sync.dma_start(wa_raw[:], wa_words[0].bitcast(I32))
         load_words(v2_tab[0], tab2_words[0])
-        load_words(v2_tab[1], tab2_words[1])
         load_wb(1, 0)
-        load_g(1)
-        load_g(2)
+        load_wb(0, 1)
+        load_words(v2_tab[1], tab2_words[1])
         load_w(1)
+        load_w(0)
         load_g(3)
         load_g(0)
-        nc.gpsimd.tensor_scalar(minus[:], gain_sb[:], 0.0, -2.0, ALU.is_lt, ALU.mult)
-        nc.gpsimd.tensor_scalar(sign[:], minus[:], 1.0, None, ALU.add)
-        nc.gpsimd.tensor_tensor(size[:], gain_sb[:], sign[:], ALU.mult)
-        nc.gpsimd.tensor_scalar(floor[:], size[:], ROOT_FLOOR, None, ALU.max)
-        nc.scalar.activation(guess[:], floor[:], ACT.Sqrt)
-        wb_g[0, 0] = round_wb(0, 0, 128)
-        g_picked[2, 0] = gather("g2_", g_tab[2][:], idx, 0, F32)
-        v2_codes[1, 0] = gather("v2_codes1", v2_tab[1][:].bitcast(U32), idx2, 0, U32)
-        v_codes[0] = gather("v_codes", v_tab[:].bitcast(U32), idx, 0, U32)
-        nc.vector.reciprocal(inverse[:], guess[:])
-        wb_g[0, 1] = round_wb(0, 1, 0)
+        load_g(1)
+        load_g(2)
+        nc.scalar.activation(size[:], gain_sb[:], ACT.Abs)
+        nc.scalar.activation(guess[:], size[:], ACT.Sqrt, bias=ROOT_FLOOR)
+        nc.vector.tensor_scalar(minus[:], gain_sb[:], 0.0, -2.0, ALU.is_lt, ALU.mult)
+        wb_g[0, 0] = round_wb(0, 0, 0)
         wb_g[1, 1] = round_wb(1, 1, 0)
+        v_codes[1] = gather("v_codes", v_tab[:].bitcast(U32), idx, 1, U32)
+        wa_sc = line.tile([P, H], U8, name="wa_sc", tag="vout", align_bytes=64)
         nc.vector.tensor_copy(
             wa_sc[:].rearrange("p (b t m) -> p b t m", t=PACK, m=P),
             wa_rows[:].bitcast(U8).rearrange("p (b m t) -> p b t m", t=PACK, m=P),
         )
-        nc.vector.scalar_tensor_tensor(half_ratio[:], size[:], 0.5, inverse[:], ALU.mult, ALU.mult)
-        wb_g[1, 0] = round_wb(1, 0, 128)
-        w_g[0] = round_w(0, "G", 0)
-        g_picked[0, 1] = gather("g0_", g_tab[0][:], idx, 1, F32)
-        w_g[1] = round_w(1, "G", 0)
-        g_picked[1, 0] = gather("g1_", g_tab[1][:], idx, 0, F32)
-        w_q[1] = quantise("w1", w_g[1])
-        wb_q[1, 1] = quantise("wb11", wb_g[1, 1])
+        v_codes[0] = gather("v_codes", v_tab[:].bitcast(U32), idx, 0, U32)
         v_sc[0] = gather("v_sc", v_rows[:].bitcast(U8), idx, 0, U8)
-        v2_sc[1] = gather("v2_sc", v2_rows[:].bitcast(U8), idx2, 1, U8)
-        g_picked[3, 1] = gather("g3_", g_tab[3][:], idx, 1, F32)
-        v2_codes[1, 1] = gather("v2_codes1", v2_tab[1][:].bitcast(U32), idx2, 1, U32)
-        v2_codes[0, 0] = gather("v2_codes0", v2_tab[0][:].bitcast(U32), idx2, 0, U32)
-        wb_q[1, 0] = quantise("wb10", wb_g[1, 0])
-        v2_codes[0, 1] = gather("v2_codes0", v2_tab[0][:].bitcast(U32), idx2, 1, U32)
-        wb_q[0, 1] = quantise("wb01", wb_g[0, 1])
+        v_sc[1] = gather("v_sc", v_rows[:].bitcast(U8), idx, 1, U8)
+        nc.vector.tensor_scalar(sign[:], minus[:], 1.0, None, ALU.add)
+        nc.vector.reciprocal(inverse[:], guess[:])
+        v2_sc[0] = gather("v2_sc", v2_rows[:].bitcast(U8), idx2, 0, U8)
+        nc.vector.scalar_tensor_tensor(half_ratio[:], size[:], 0.5, inverse[:], ALU.mult, ALU.mult)
+        wa_codes = line.tile([P, 2 * H], U8, name="wa_codes", tag="vout", align_bytes=64)
         nc.vector.tensor_copy(
             wa_codes[:].bitcast(U16).rearrange("p (b t m) -> p b t m", t=PACK, m=P),
             wa_raw[:].bitcast(U16).rearrange("p (b m t) -> p b t m", t=PACK, m=P),
         )
-        v2_sc[0] = gather("v2_sc", v2_rows[:].bitcast(U8), idx2, 0, U8)
-        g_picked[2, 1] = gather("g2_", g_tab[2][:], idx, 1, F32)
-        v_sc[1] = gather("v_sc", v_rows[:].bitcast(U8), idx, 1, U8)
-        nc.vector.scalar_tensor_tensor(root[:], guess[:], 0.5, half_ratio[:], ALU.mult, ALU.add)
-        h_p[1, 0] = factors(1, 0)
         wb_q[0, 0] = quantise("wb00", wb_g[0, 0])
-        v_codes[1] = gather("v_codes", v_tab[:].bitcast(U32), idx, 1, U32)
-        h_p[1, 1] = factors(1, 1)
+        wb_g[1, 0] = round_wb(1, 0, 0)
+        wb_q[1, 1] = quantise("wb11", wb_g[1, 1])
+        wb_g[0, 1] = round_wb(0, 1, 0)
+        v2_codes[0, 0] = gather("v2_codes0", v2_tab[0][:].bitcast(U32), idx2, 0, U32)
+        v2_codes[0, 1] = gather("v2_codes0", v2_tab[0][:].bitcast(U32), idx2, 1, U32)
+        v2_sc[1] = gather("v2_sc", v2_rows[:].bitcast(U8), idx2, 1, U8)
+        wb_q[1, 0] = quantise("wb10", wb_g[1, 0])
+        v2_codes[1, 1] = gather("v2_codes1", v2_tab[1][:].bitcast(U32), idx2, 1, U32)
+        v2_codes[1, 0] = gather("v2_codes1", v2_tab[1][:].bitcast(U32), idx2, 0, U32)
+        wb_q[0, 1] = quantise("wb01", wb_g[0, 1])
+        nc.vector.scalar_tensor_tensor(root[:], guess[:], 0.5, half_ratio[:], ALU.mult, ALU.add)
         h_p[0, 1] = factors(0, 1)
-        w_q[0] = quantise("w0", w_g[0])
-        h_g[1, 0] = interleave(h_p[1, 0], 96)
-        h_g[1, 1] = interleave(h_p[1, 1], 96)
-        h_q[1, 1] = quantise("h11", h_g[1, 1])
-        h_g[0, 1] = interleave(h_p[0, 1], 32)
+        h_g[0, 1] = interleave(h_p[0, 1], 0)
+        w_g[1] = round_w(1, "V", 128)
         h_p[0, 0] = factors(0, 0)
+        w_g[0] = round_w(0, "V", 64)
+        w_q[1] = quantise("w1", w_g[1])
         h_g[0, 0] = interleave(h_p[0, 0], 0)
-        g_picked[3, 0] = gather("g3_", g_tab[3][:], idx, 0, F32)
+        h_p[1, 0] = factors(1, 0)
+        g_picked[3, 1] = gather("g3_", g_tab[3][:], idx, 1, F32)
+        h_g[1, 0] = interleave(h_p[1, 0], 0)
+        g_picked[0, 1] = gather("g0_", g_tab[0][:], idx, 1, F32)
         h_q[0, 1] = quantise("h01", h_g[0, 1])
-        finish(3, 1)
-        g_picked[1, 1] = gather("g1_", g_tab[1][:], idx, 1, F32)
-        h_q[1, 0] = quantise("h10", h_g[1, 0])
-        h_q[0, 0] = quantise("h00", h_g[0, 0])
-        finish(1, 0)
-        finish(2, 0)
+        h_p[1, 1] = factors(1, 1)
+        w_q[0] = quantise("w0", w_g[0])
         g_picked[0, 0] = gather("g0_", g_tab[0][:], idx, 0, F32)
-        finish(0, 1)
-        finish(1, 1)
+        g_picked[3, 0] = gather("g3_", g_tab[3][:], idx, 0, F32)
+        h_q[0, 0] = quantise("h00", h_g[0, 0])
+        g_picked[1, 0] = gather("g1_", g_tab[1][:], idx, 0, F32)
+        g_picked[1, 1] = gather("g1_", g_tab[1][:], idx, 1, F32)
+        h_g[1, 1] = interleave(h_p[1, 1], 0)
+        h_q[1, 0] = quantise("h10", h_g[1, 0])
+        g_picked[2, 1] = gather("g2_", g_tab[2][:], idx, 1, F32)
+        g_picked[2, 0] = gather("g2_", g_tab[2][:], idx, 0, F32)
+        finish(1, 0)
+        finish(3, 0)
+        h_q[1, 1] = quantise("h11", h_g[1, 1])
         finish(0, 0)
         finish(2, 1)
-        finish(3, 0)
+        finish(3, 1)
+        finish(0, 1)
+        finish(1, 1)
+        finish(2, 0)

@@ -58,6 +58,10 @@ def tile_list_squared_factor_match_kernel(
 
         def load_scales(tile, rows, first, queue):
             passes = rows.shape[0]
+            if passes == 1:
+                for r in range(4):
+                    queue.dma_start(tile[r:P:32, :], rows.bitcast(I32)[0, r:16:4, :])
+                return
             for q in range(4):
                 lo = 32 * q + first
                 queue.dma_start(tile[lo : lo + 4 * passes, :], rows.bitcast(I32)[:, 4 * q : 4 * q + 4, :])
@@ -89,6 +93,12 @@ def tile_list_squared_factor_match_kernel(
             if on_vector < P:
                 nc.scalar.copy(out=dst[:, on_vector:], in_=src[:, on_vector:])
 
+        def pool_copy(grouped, planes):
+            dst = grouped[:].rearrange("p (c t) -> p c t", t=PACK)
+            src = planes[:].rearrange("p t c -> p c t")
+            for c in range(0, COLS, P):
+                nc.gpsimd.tensor_scalar(dst[:, c : c + P], src[:, c : c + P], 1.0, 0.0, ALU.mult, ALU.add)
+
         def round_wb(a, b, on_vector):
             grouped = ring.tile([P, PACK * PASS], BF16, name="grouped", tag="stage", align_bytes=64)
             shared_copy(
@@ -110,10 +120,16 @@ def tile_list_squared_factor_match_kernel(
                 return grouped
             signed = ring.tile([P, PACK, N], BF16, name="signed", tag="stage", align_bytes=64)
             for j in range(PACK):
-                nc.scalar.activation(signed[:, j, :], w_raw[b][:, j, :], ACT.Copy, scale=sign[:, b, j : j + 1])
+                if how == "G":
+                    nc.gpsimd.tensor_scalar(signed[:, j, :], w_raw[b][:, j, :], sign[:, b, j : j + 1], 0.0, ALU.mult, ALU.add)
+                else:
+                    nc.scalar.activation(signed[:, j, :], w_raw[b][:, j, :], ACT.Copy, scale=sign[:, b, j : j + 1])
             grouped = ring.tile([P, PACK * N], BF16, name="grouped", tag="stage", align_bytes=64)
             dst = grouped[:].rearrange("p (c i j) -> p c j i", i=4, j=PACK)
-            shared_copy(dst, signed[:].rearrange("p j (c i) -> p c j i", i=4), on_vector)
+            if on_vector > P:
+                pool_copy(grouped, signed)
+            else:
+                shared_copy(dst, signed[:].rearrange("p j (c i) -> p c j i", i=4), on_vector)
             return grouped
 
         def factors(b, jh):
@@ -148,7 +164,10 @@ def tile_list_squared_factor_match_kernel(
             grouped = ring.tile([P, PACK * COLS], BF16, name="h_grouped", tag="stage", align_bytes=64)
             dst = grouped[:].rearrange("p (c i t) -> p c t i", i=4, t=PACK)
             src = planes[:].rearrange("p t (c i) -> p c t i", i=4)
-            shared_copy(dst, src, on_vector)
+            if on_vector > P:
+                pool_copy(grouped, planes)
+            else:
+                shared_copy(dst, src, on_vector)
             return grouped
 
         def finish(n, jh):
@@ -181,90 +200,90 @@ def tile_list_squared_factor_match_kernel(
         nc.vector.memset(v_rows[:], 0)
         nc.vector.memset(v2_rows[:], 0)
         nc.vector.memset(wa_rows[:], 0)
-        nc.sync.dma_start(idx[:], offs)
-        nc.sync.dma_start(gain_sb[:], gain.rearrange("(b p t) -> p b t", p=P, t=PACK))
-        load_scales(wa_rows, wa_scales, 0, nc.sync)
-        load_words(v_tab, tab_words[0])
-        load_wb(1, 1)
-        load_scales(v_rows, tab_scales, 0, nc.sync)
-        load_wb(0, 0)
         nc.sync.dma_start(idx2[:], offs2)
-        load_scales(v2_rows, tab2_scales, 4, nc.sync)
-        nc.sync.dma_start(wa_raw[:], wa_words[0].bitcast(I32))
+        nc.sync.dma_start(gain_sb[:], gain.rearrange("(b p t) -> p b t", p=P, t=PACK))
+        nc.sync.dma_start(idx[:], offs)
         load_words(v2_tab[0], tab2_words[0])
-        load_wb(1, 0)
-        load_wb(0, 1)
+        load_scales(v_rows, tab_scales, 0, nc.sync)
+        load_words(v_tab, tab_words[0])
+        load_wb(0, 0)
+        load_scales(wa_rows, wa_scales, 0, nc.sync)
         load_words(v2_tab[1], tab2_words[1])
-        load_w(1)
         load_w(0)
-        load_g(3)
+        nc.sync.dma_start(wa_raw[:], wa_words[0].bitcast(I32))
+        load_wb(1, 0)
+        load_scales(v2_rows, tab2_scales, 4, nc.sync)
+        load_wb(0, 1)
         load_g(0)
+        load_wb(1, 1)
         load_g(1)
+        load_w(1)
         load_g(2)
+        load_g(3)
         nc.scalar.activation(size[:], gain_sb[:], ACT.Abs)
         nc.scalar.activation(guess[:], size[:], ACT.Sqrt, bias=ROOT_FLOOR)
         nc.vector.tensor_scalar(minus[:], gain_sb[:], 0.0, -2.0, ALU.is_lt, ALU.mult)
-        wb_g[0, 0] = round_wb(0, 0, 0)
-        wb_g[1, 1] = round_wb(1, 1, 0)
+        v2_codes[0, 1] = gather("v2_codes0", v2_tab[0][:].bitcast(U32), idx2, 1, U32)
+        v_sc[0] = gather("v_sc", v_rows[:].bitcast(U8), idx, 0, U8)
+        v2_codes[0, 0] = gather("v2_codes0", v2_tab[0][:].bitcast(U32), idx2, 0, U32)
+        v_sc[1] = gather("v_sc", v_rows[:].bitcast(U8), idx, 1, U8)
+        v_codes[0] = gather("v_codes", v_tab[:].bitcast(U32), idx, 0, U32)
         v_codes[1] = gather("v_codes", v_tab[:].bitcast(U32), idx, 1, U32)
+        v2_codes[1, 1] = gather("v2_codes1", v2_tab[1][:].bitcast(U32), idx2, 1, U32)
+        wb_g[0, 0] = round_wb(0, 0, 0)
+        nc.vector.tensor_scalar(sign[:], minus[:], 1.0, None, ALU.add)
+        nc.vector.reciprocal(inverse[:], guess[:])
+        w_g[0] = round_w(0, "S", 64)
+        nc.vector.scalar_tensor_tensor(half_ratio[:], size[:], 0.5, inverse[:], ALU.mult, ALU.mult)
         wa_sc = line.tile([P, H], U8, name="wa_sc", tag="vout", align_bytes=64)
         nc.vector.tensor_copy(
             wa_sc[:].rearrange("p (b t m) -> p b t m", t=PACK, m=P),
             wa_rows[:].bitcast(U8).rearrange("p (b m t) -> p b t m", t=PACK, m=P),
         )
-        v_codes[0] = gather("v_codes", v_tab[:].bitcast(U32), idx, 0, U32)
-        v_sc[0] = gather("v_sc", v_rows[:].bitcast(U8), idx, 0, U8)
-        v_sc[1] = gather("v_sc", v_rows[:].bitcast(U8), idx, 1, U8)
-        nc.vector.tensor_scalar(sign[:], minus[:], 1.0, None, ALU.add)
-        nc.vector.reciprocal(inverse[:], guess[:])
-        v2_sc[0] = gather("v2_sc", v2_rows[:].bitcast(U8), idx2, 0, U8)
-        nc.vector.scalar_tensor_tensor(half_ratio[:], size[:], 0.5, inverse[:], ALU.mult, ALU.mult)
         wa_codes = line.tile([P, 2 * H], U8, name="wa_codes", tag="vout", align_bytes=64)
         nc.vector.tensor_copy(
             wa_codes[:].bitcast(U16).rearrange("p (b t m) -> p b t m", t=PACK, m=P),
             wa_raw[:].bitcast(U16).rearrange("p (b m t) -> p b t m", t=PACK, m=P),
         )
-        wb_q[0, 0] = quantise("wb00", wb_g[0, 0])
-        wb_g[1, 0] = round_wb(1, 0, 0)
-        wb_q[1, 1] = quantise("wb11", wb_g[1, 1])
-        wb_g[0, 1] = round_wb(0, 1, 0)
-        v2_codes[0, 0] = gather("v2_codes0", v2_tab[0][:].bitcast(U32), idx2, 0, U32)
-        v2_codes[0, 1] = gather("v2_codes0", v2_tab[0][:].bitcast(U32), idx2, 1, U32)
-        v2_sc[1] = gather("v2_sc", v2_rows[:].bitcast(U8), idx2, 1, U8)
-        wb_q[1, 0] = quantise("wb10", wb_g[1, 0])
-        v2_codes[1, 1] = gather("v2_codes1", v2_tab[1][:].bitcast(U32), idx2, 1, U32)
-        v2_codes[1, 0] = gather("v2_codes1", v2_tab[1][:].bitcast(U32), idx2, 0, U32)
-        wb_q[0, 1] = quantise("wb01", wb_g[0, 1])
         nc.vector.scalar_tensor_tensor(root[:], guess[:], 0.5, half_ratio[:], ALU.mult, ALU.add)
-        h_p[0, 1] = factors(0, 1)
-        h_g[0, 1] = interleave(h_p[0, 1], 0)
-        w_g[1] = round_w(1, "V", 128)
-        h_p[0, 0] = factors(0, 0)
-        w_g[0] = round_w(0, "V", 64)
-        w_q[1] = quantise("w1", w_g[1])
-        h_g[0, 0] = interleave(h_p[0, 0], 0)
-        h_p[1, 0] = factors(1, 0)
-        g_picked[3, 1] = gather("g3_", g_tab[3][:], idx, 1, F32)
-        h_g[1, 0] = interleave(h_p[1, 0], 0)
-        g_picked[0, 1] = gather("g0_", g_tab[0][:], idx, 1, F32)
-        h_q[0, 1] = quantise("h01", h_g[0, 1])
-        h_p[1, 1] = factors(1, 1)
+        wb_g[1, 0] = round_wb(1, 0, 0)
+        wb_q[0, 0] = quantise("wb00", wb_g[0, 0])
+        v2_codes[1, 0] = gather("v2_codes1", v2_tab[1][:].bitcast(U32), idx2, 0, U32)
+        v2_sc[0] = gather("v2_sc", v2_rows[:].bitcast(U8), idx2, 0, U8)
+        v2_sc[1] = gather("v2_sc", v2_rows[:].bitcast(U8), idx2, 1, U8)
+        wb_g[0, 1] = round_wb(0, 1, 0)
+        wb_q[1, 0] = quantise("wb10", wb_g[1, 0])
         w_q[0] = quantise("w0", w_g[0])
         g_picked[0, 0] = gather("g0_", g_tab[0][:], idx, 0, F32)
-        g_picked[3, 0] = gather("g3_", g_tab[3][:], idx, 0, F32)
-        h_q[0, 0] = quantise("h00", h_g[0, 0])
+        h_p[0, 0] = factors(0, 0)
+        wb_q[0, 1] = quantise("wb01", wb_g[0, 1])
+        g_picked[0, 1] = gather("g0_", g_tab[0][:], idx, 1, F32)
+        h_p[0, 1] = factors(0, 1)
         g_picked[1, 0] = gather("g1_", g_tab[1][:], idx, 0, F32)
+        h_g[0, 0] = interleave(h_p[0, 0], 32)
+        wb_g[1, 1] = round_wb(1, 1, 128)
+        h_g[0, 1] = interleave(h_p[0, 1], 0)
+        wb_q[1, 1] = quantise("wb11", wb_g[1, 1])
+        h_p[1, 0] = factors(1, 0)
         g_picked[1, 1] = gather("g1_", g_tab[1][:], idx, 1, F32)
-        h_g[1, 1] = interleave(h_p[1, 1], 0)
-        h_q[1, 0] = quantise("h10", h_g[1, 0])
+        w_g[1] = round_w(1, "V", 32)
         g_picked[2, 1] = gather("g2_", g_tab[2][:], idx, 1, F32)
+        w_q[1] = quantise("w1", w_g[1])
         g_picked[2, 0] = gather("g2_", g_tab[2][:], idx, 0, F32)
-        finish(1, 0)
+        h_g[1, 0] = interleave(h_p[1, 0], 0)
+        h_q[0, 0] = quantise("h00", h_g[0, 0])
+        g_picked[3, 0] = gather("g3_", g_tab[3][:], idx, 0, F32)
+        h_q[1, 0] = quantise("h10", h_g[1, 0])
+        h_p[1, 1] = factors(1, 1)
         finish(3, 0)
-        h_q[1, 1] = quantise("h11", h_g[1, 1])
-        finish(0, 0)
-        finish(2, 1)
-        finish(3, 1)
-        finish(0, 1)
-        finish(1, 1)
+        h_q[0, 1] = quantise("h01", h_g[0, 1])
+        g_picked[3, 1] = gather("g3_", g_tab[3][:], idx, 1, F32)
         finish(2, 0)
+        h_g[1, 1] = interleave(h_p[1, 1], 0)
+        finish(1, 0)
+        h_q[1, 1] = quantise("h11", h_g[1, 1])
+        finish(1, 1)
+        finish(2, 1)
+        finish(0, 0)
+        finish(0, 1)
+        finish(3, 1)

from contextlib import ExitStack

import concourse.mybir as mybir

K, K2, H, N, T, S = 512, 1024, 1024, 512, 2048, 1024
FLOPS = 2 * S * (K * H + K2 * H + H * N)

F32 = mybir.dt.float32
BF16 = mybir.dt.bfloat16
I32 = mybir.dt.int32
U32 = mybir.dt.uint32
U16 = mybir.dt.uint16
U8 = mybir.dt.uint8
FP8X4 = mybir.dt.float8_e4m3fn_x4
FP4X4 = mybir.dt.float4_e2m1fn_x4
ALU = mybir.AluOpType
ACT = mybir.ActivationFunctionType

P = 128
PACK = 4
PASS = P * PACK
COLS = 512
HALVES = S // COLS
ROOT_FLOOR = 2.0**-100


def tile_list_squared_factor_match_kernel(
    tc, tab_words, tab_scales, tab2_words, tab2_scales, wa_words, wa_scales, wb, gain, w, gT, offs, offs2, out
):
    nc = tc.nc
    with ExitStack() as ctx:
        keep = ctx.enter_context(tc.tile_pool(name="keep", bufs=1))
        ring = ctx.enter_context(tc.tile_pool(name="ring", bufs=12))
        line = ctx.enter_context(tc.tile_pool(name="line", bufs=30))
        psum = ctx.enter_context(tc.psum_pool(name="psum", bufs=8))

        def held(name, shape, dtype):
            return keep.tile(shape, dtype, name=name, align_bytes=64)

        idx = held("idx", [P, S // 16], U16)
        idx2 = held("idx2", [P, S // 16], U16)
        gain_sb = held("gain_sb", [P, H // PASS, PACK], F32)
        v_rows = held("v_rows", [P, T // 4], I32)
        v2_rows = held("v2_rows", [P, T // 4], I32)
        wa_rows = held("wa_rows", [P, H // 4], I32)
        v_tab = held("v_tab", [P, T], I32)
        v2_tab = [held(f"v2_tab{a}", [P, T], I32) for a in range(2)]
        wa_raw = held("wa_raw", [P, H // 2], I32)
        wb_raw = {(a, b): held(f"wb_raw{a}{b}", [P, PACK, PASS], F32) for a in range(2) for b in range(2)}
        w_raw = [held(f"w_raw{b}", [P, PACK, N], F32) for b in range(2)]
        g_tab = [held(f"g_tab{n}", [P, T], F32) for n in range(4)]

        def half_of(offsets, jh):
            return offsets[:, jh * (COLS // 16) : (jh + 1) * (COLS // 16)]

        def load_words(tile, words):
            nc.sync.dma_start(tile[:], words.rearrange("p n t -> p (n t)").bitcast(I32))

        def load_scales(tile, rows, first, queue):
            passes = rows.shape[0]
            if passes == 1:
                for r in range(4):
                    queue.dma_start(tile[r:P:32, :], rows.bitcast(I32)[0, r:16:4, :])
                return
            for q in range(4):
                lo = 32 * q + first
                queue.dma_start(tile[lo : lo + 4 * passes, :], rows.bitcast(I32)[:, 4 * q : 4 * q + 4, :])

        def load_wb(a, b):
            rows = wb[a * PASS : (a + 1) * PASS, b * PASS : (b + 1) * PASS]
            nc.sync.dma_start(wb_raw[a, b][:], rows.rearrange("(p j) c -> p j c", j=PACK))

        def load_w(b):
            nc.sync.dma_start(w_raw[b][:], w[b * PASS : (b + 1) * PASS, :].rearrange("(p j) c -> p j c", j=PACK))

        def load_g(n):
            nc.sync.dma_start(g_tab[n][:], gT[n * P : (n + 1) * P, :])

        def gather(name, window, offsets, jh, dtype):
            tile = line.tile([P, COLS], dtype, name=f"{name}{jh}", tag="vout", align_bytes=64)
            nc.vector.tensor_copy(tile[:], window.indirect(half_of(offsets, jh)))
            return tile

        def quantise(name, grouped):
            codes = line.tile([P, COLS], U32, name=name + "_codes", tag="vout", align_bytes=64)
            scales = held(name + "_scales", [P, COLS], U8)
            nc.vector.quantize_mx(out=codes[:].bitcast(FP8X4), scales=scales[:], in_=grouped[:])
            return codes, scales

        def shared_copy(dst, src, on_vector):
            if on_vector > 0:
                nc.vector.tensor_copy(dst[:, :on_vector], src[:, :on_vector])
            if on_vector < P:
                nc.scalar.copy(out=dst[:, on_vector:], in_=src[:, on_vector:])

        def pool_copy(grouped, planes):
            dst = grouped[:].rearrange("p (c t) -> p c t", t=PACK)
            src = planes[:].rearrange("p t c -> p c t")
            for c in range(0, COLS, P):
                nc.gpsimd.tensor_scalar(dst[:, c : c + P], src[:, c : c + P], 1.0, 0.0, ALU.mult, ALU.add)

        def round_wb(a, b, on_vector):
            grouped = ring.tile([P, PACK * PASS], BF16, name="grouped", tag="stage", align_bytes=64)
            shared_copy(
                grouped[:].rearrange("p (t m j) -> p m j t", t=PACK, j=PACK),
                wb_raw[a, b][:].rearrange("p j (m t) -> p m j t", t=PACK),
                on_vector,
            )
            return grouped

        def round_w(b, how, on_vector):
            if how == "V":
                grouped = ring.tile([P, PACK * N], BF16, name="grouped", tag="stage", align_bytes=64)
                nc.vector.tensor_tensor(
                    grouped[:].rearrange("p (c i j) -> p c j i", i=4, j=PACK),
                    w_raw[b][:].rearrange("p j (c i) -> p c j i", i=4),
                    sign[:, b, :].unsqueeze(1).unsqueeze(3).to_broadcast([P, N // 4, PACK, 4]),
                    ALU.mult,
                )
                return grouped
            signed = ring.tile([P, PACK, N], BF16, name="signed", tag="stage", align_bytes=64)
            for j in range(PACK):
                if how == "G":
                    nc.gpsimd.tensor_scalar(signed[:, j, :], w_raw[b][:, j, :], sign[:, b, j : j + 1], 0.0, ALU.mult, ALU.add)
                else:
                    nc.scalar.activation(signed[:, j, :], w_raw[b][:, j, :], ACT.Copy, scale=sign[:, b, j : j + 1])
            grouped = ring.tile([P, PACK * N], BF16, name="grouped", tag="stage", align_bytes=64)
            dst = grouped[:].rearrange("p (c i j) -> p c j i", i=4, j=PACK)
            if on_vector > P:
                pool_copy(grouped, signed)
            else:
                shared_copy(dst, signed[:].rearrange("p j (c i) -> p c j i", i=4), on_vector)
            return grouped

        def factors(b, jh):
            planes = ring.tile([P, PACK, COLS], BF16, name="planes", tag="stage", align_bytes=64)
            for t in range(PACK):
                acc = psum.tile([P, COLS], F32, name="acc")
                col = (b * PACK + t) * P
                nc.tensor.matmul_mx(
                    out=acc[:],
                    lhsT=wa_codes[:, 2 * col : 2 * (col + P)].bitcast(FP4X4),
                    lhsT_scale=wa_sc[:, col : col + P],
                    rhs=v_codes[jh][:].bitcast(FP8X4),
                    rhs_scale=v_sc[jh][:],
                    start=True,
                    stop=False,
                )
                for a in range(2):
                    codes, scales = wb_q[a, b]
                    nc.tensor.matmul_mx(
                        out=acc[:],
                        lhsT=codes[:, t * P : (t + 1) * P].bitcast(FP8X4),
                        lhsT_scale=scales[:, t * P : (t + 1) * P],
                        rhs=v2_codes[a, jh][:].bitcast(FP8X4),
                        rhs_scale=v2_sc[jh][4 + 4 * a :, :],
                        start=False,
                        stop=(a == 1),
                    )
                nc.scalar.activation(planes[:, t, :], acc[:], ACT.Square, scale=root[:, b, t : t + 1])
            return planes

        def interleave(planes, on_vector):
            grouped = ring.tile([P, PACK * COLS], BF16, name="h_grouped", tag="stage", align_bytes=64)
            dst = grouped[:].rearrange("p (c i t) -> p c t i", i=4, t=PACK)
            src = planes[:].rearrange("p t (c i) -> p c t i", i=4)
            if on_vector > P:
                pool_copy(grouped, planes)
            else:
                shared_copy(dst, src, on_vector)
            return grouped

        def finish(n, jh):
            acc = psum.tile([P, COLS], F32, name="acc")
            for b in range(2):
                w_codes, w_scales = w_q[b]
                h_codes, h_scales = h_q[b, jh]
                nc.tensor.matmul_mx(
                    out=acc[:],
                    lhsT=w_codes[:, n * P : (n + 1) * P].bitcast(FP8X4),
                    lhsT_scale=w_scales[:, n * P : (n + 1) * P],
                    rhs=h_codes[:].bitcast(FP8X4),
                    rhs_scale=h_scales[:],
                    start=(b == 0),
                    stop=(b == 1),
                )
            result = g_picked[n, jh]
            nc.vector.tensor_tensor(result[:], acc[:], result[:], ALU.subtract)
            nc.sync.dma_start(out[n * P : (n + 1) * P, jh * COLS : (jh + 1) * COLS], result[:])

        shape = [P, H // PASS, PACK]
        sign = held("sign", shape, F32)
        minus = held("minus", shape, F32)
        size = held("size", shape, F32)
        guess = held("guess", shape, F32)
        inverse = held("inverse", shape, F32)
        half_ratio = held("half_ratio", shape, F32)
        root = held("root", shape, F32)
        v_sc, v_codes, v2_sc, v2_codes, wb_q, w_q, h_q, g_picked, wb_g, w_g, h_p, h_g = ({} for each in range(12))
        nc.vector.memset(v_rows[:], 0)
        nc.vector.memset(v2_rows[:], 0)
        nc.vector.memset(wa_rows[:], 0)
        nc.sync.dma_start(idx2[:], offs2)
        nc.sync.dma_start(gain_sb[:], gain.rearrange("(b p t) -> p b t", p=P, t=PACK))
        nc.sync.dma_start(idx[:], offs)
        load_words(v2_tab[0], tab2_words[0])
        load_scales(v_rows, tab_scales, 0, nc.sync)
        load_words(v_tab, tab_words[0])
        load_wb(0, 0)
        load_scales(wa_rows, wa_scales, 0, nc.sync)
        load_words(v2_tab[1], tab2_words[1])
        load_w(0)
        nc.sync.dma_start(wa_raw[:], wa_words[0].bitcast(I32))
        load_wb(1, 0)
        load_scales(v2_rows, tab2_scales, 4, nc.sync)
        load_wb(0, 1)
        load_g(0)
        load_wb(1, 1)
        load_g(1)
        load_w(1)
        load_g(2)
        load_g(3)
        nc.scalar.activation(size[:], gain_sb[:], ACT.Abs)
        nc.scalar.activation(guess[:], size[:], ACT.Sqrt, bias=ROOT_FLOOR)
        nc.vector.tensor_scalar(minus[:], gain_sb[:], 0.0, -2.0, ALU.is_lt, ALU.mult)
        v2_codes[0, 1] = gather("v2_codes0", v2_tab[0][:].bitcast(U32), idx2, 1, U32)
        v_sc[0] = gather("v_sc", v_rows[:].bitcast(U8), idx, 0, U8)
        v2_codes[0, 0] = gather("v2_codes0", v2_tab[0][:].bitcast(U32), idx2, 0, U32)
        v_sc[1] = gather("v_sc", v_rows[:].bitcast(U8), idx, 1, U8)
        v_codes[0] = gather("v_codes", v_tab[:].bitcast(U32), idx, 0, U32)
        v_codes[1] = gather("v_codes", v_tab[:].bitcast(U32), idx, 1, U32)
        v2_codes[1, 1] = gather("v2_codes1", v2_tab[1][:].bitcast(U32), idx2, 1, U32)
        wb_g[0, 0] = round_wb(0, 0, 0)
        nc.vector.tensor_scalar(sign[:], minus[:], 1.0, None, ALU.add)
        nc.vector.reciprocal(inverse[:], guess[:])
        w_g[0] = round_w(0, "S", 64)
        nc.vector.scalar_tensor_tensor(half_ratio[:], size[:], 0.5, inverse[:], ALU.mult, ALU.mult)
        wa_sc = line.tile([P, H], U8, name="wa_sc", tag="vout", align_bytes=64)
        nc.vector.tensor_copy(
            wa_sc[:].rearrange("p (b t m) -> p b t m", t=PACK, m=P),
            wa_rows[:].bitcast(U8).rearrange("p (b m t) -> p b t m", t=PACK, m=P),
        )
        wa_codes = line.tile([P, 2 * H], U8, name="wa_codes", tag="vout", align_bytes=64)
        nc.vector.tensor_copy(
            wa_codes[:].bitcast(U16).rearrange("p (b t m) -> p b t m", t=PACK, m=P),
            wa_raw[:].bitcast(U16).rearrange("p (b m t) -> p b t m", t=PACK, m=P),
        )
        nc.vector.scalar_tensor_tensor(root[:], guess[:], 0.5, half_ratio[:], ALU.mult, ALU.add)
        wb_g[1, 0] = round_wb(1, 0, 0)
        wb_q[0, 0] = quantise("wb00", wb_g[0, 0])
        v2_codes[1, 0] = gather("v2_codes1", v2_tab[1][:].bitcast(U32), idx2, 0, U32)
        v2_sc[0] = gather("v2_sc", v2_rows[:].bitcast(U8), idx2, 0, U8)
        v2_sc[1] = gather("v2_sc", v2_rows[:].bitcast(U8), idx2, 1, U8)
        wb_g[0, 1] = round_wb(0, 1, 0)
        wb_q[1, 0] = quantise("wb10", wb_g[1, 0])
        w_q[0] = quantise("w0", w_g[0])
        g_picked[0, 0] = gather("g0_", g_tab[0][:], idx, 0, F32)
        h_p[0, 0] = factors(0, 0)
        wb_q[0, 1] = quantise("wb01", wb_g[0, 1])
        g_picked[0, 1] = gather("g0_", g_tab[0][:], idx, 1, F32)
        h_p[0, 1] = factors(0, 1)
        g_picked[1, 0] = gather("g1_", g_tab[1][:], idx, 0, F32)
        h_g[0, 0] = interleave(h_p[0, 0], 32)
        wb_g[1, 1] = round_wb(1, 1, 128)
        h_g[0, 1] = interleave(h_p[0, 1], 0)
        wb_q[1, 1] = quantise("wb11", wb_g[1, 1])
        h_p[1, 0] = factors(1, 0)
        g_picked[1, 1] = gather("g1_", g_tab[1][:], idx, 1, F32)
        w_g[1] = round_w(1, "V", 32)
        g_picked[2, 1] = gather("g2_", g_tab[2][:], idx, 1, F32)
        w_q[1] = quantise("w1", w_g[1])
        g_picked[2, 0] = gather("g2_", g_tab[2][:], idx, 0, F32)
        h_g[1, 0] = interleave(h_p[1, 0], 0)
        h_q[0, 0] = quantise("h00", h_g[0, 0])
        g_picked[3, 0] = gather("g3_", g_tab[3][:], idx, 0, F32)
        h_q[1, 0] = quantise("h10", h_g[1, 0])
        h_p[1, 1] = factors(1, 1)
        finish(3, 0)
        h_q[0, 1] = quantise("h01", h_g[0, 1])
        g_picked[3, 1] = gather("g3_", g_tab[3][:], idx, 1, F32)
        finish(2, 0)
        h_g[1, 1] = interleave(h_p[1, 1], 0)
        finish(1, 0)
        h_q[1, 1] = quantise("h11", h_g[1, 1])
        finish(1, 1)
        finish(2, 1)
        finish(0, 0)
        finish(0, 1)
        finish(3, 1)
